import numpy as np
import ml_dtypes


def mxq(x, axis, fmt="e4m3"):
    dtype, down = {"e4m3": (ml_dtypes.float8_e4m3fn, 7), "e5m2": (ml_dtypes.float8_e5m2, 14)}[fmt]
    v = np.moveaxis(np.asarray(x, np.float32).astype(ml_dtypes.bfloat16).astype(np.float64), axis, -1)
    blocks = v.reshape(v.shape[:-1] + (-1, 32))
    amax = np.abs(blocks).max(-1, keepdims=True)
    byte = np.maximum(np.where(amax > 0, np.frexp(amax)[1] - 1 + 127, 0) - down, 1)
    scale = np.exp2(byte - 127.0)
    codes = (blocks / scale).astype(np.float32).astype(dtype).astype(np.float64)
    return np.moveaxis((codes * scale).reshape(v.shape), -1, axis)


WIDE = False


def mx_kscale(k):
    if not WIDE:
        return np.ones(k)
    levels = np.array([10, -10, 5, -5, 0])
    if k % 512:
        return np.exp2(np.random.permutation(np.resize(levels, k // 32))).repeat(32)
    a = np.empty((k // 512, 16))
    for p in range(k // 512):
        a[p, :8] = np.random.permutation(np.resize(levels, 8))
        for g in range(8):
            far = levels[np.abs(levels - a[p, g]) >= 10]
            a[p, g + 8] = far[np.random.randint(len(far))]
    return np.exp2(a.ravel()).repeat(32)


def f64(x):
    return np.asarray(x).astype(np.float64)


def striped(idx):
    return np.tile(np.asarray(idx).reshape(-1, 16).T, (8, 1)).astype(np.uint16)


def unstriped(offs):
    return offs[:16].T.reshape(-1).astype(np.int64)


E2M1 = np.array([0.0, 0.5, 1.0, 1.5, 2.0, 3.0, 4.0, 6.0, -0.0, -0.5, -1.0, -1.5, -2.0, -3.0, -4.0, -6.0])


def pack_weight(w, fmt):
    k, n = w.shape
    w = f64(np.asarray(w, np.float32).astype(ml_dtypes.bfloat16)).reshape(k // 32, 32, n)
    amax = np.abs(w).max(1)
    if fmt == "e4m3":
        byte = np.frexp(amax)[1] - 1 + 127 - 7
    else:
        mant, ex = np.frexp(amax / 6.0)
        byte = np.where(mant > 0.5, ex, ex - 1) + 127
    byte = np.clip(np.where(amax > 0, byte, 1), 1, 254)
    scaled = (w * np.exp2(127.0 - byte)[:, None, :]).reshape(k, n).astype(np.float32)
    by_word = np.ascontiguousarray(scaled.reshape(k // 512, 128, 4, n).transpose(0, 1, 3, 2))
    if fmt == "e4m3":
        words = by_word.astype(ml_dtypes.float8_e4m3fn).view(np.uint8)
    else:
        c = by_word.astype(ml_dtypes.float4_e2m1fn).view(np.uint8) & 0xF
        words = (c[..., 0::2] | (c[..., 1::2] << 4)).reshape(k // 512, 128, 2 * n)
    return np.ascontiguousarray(words), np.ascontiguousarray(byte.astype(np.uint8).reshape(k // 512, 16, n))


def unpack_weight(words, scales, fmt):
    g, _, n = scales.shape
    words = np.ascontiguousarray(words).reshape(g, 128, n, -1)
    if fmt == "e4m3":
        vals = words.view(ml_dtypes.float8_e4m3fn).astype(np.float64)
    else:
        nib = np.empty((g, 128, n, 4), np.uint8)
        nib[..., 0::2] = words & 0xF
        nib[..., 1::2] = words >> 4
        vals = E2M1[nib]
    vals = vals * np.repeat(np.exp2(scales.astype(np.float64) - 127.0), 8, axis=1)[..., None]
    return vals.transpose(0, 1, 3, 2).reshape(g * 512, n)


def sigmoid(v):
    return 1.0 / (1.0 + np.exp(-v))


def bf(x):
    return np.asarray(x, np.float32).astype(ml_dtypes.bfloat16)


def planes(Y):
    r, m = Y.shape
    b = f64(bf(Y)).reshape(r // 32, 32, m)
    amax = np.abs(b).max(1)
    byte = np.clip(np.where(amax > 0, np.frexp(amax)[1] - 1 + 127 - 7, 1), 1, 254)
    codes = (b * np.exp2(127.0 - byte)[:, None, :]).reshape(r, m).astype(np.float32).astype(ml_dtypes.float8_e4m3fn).view(np.uint8)
    words = codes.reshape(r // 512, 128, 4, m).transpose(0, 1, 3, 2)
    return np.ascontiguousarray(words), np.ascontiguousarray(byte.astype(np.uint8).reshape(r // 512, 16, m))


K, R, F, T, J = 512, 512, 512, 2048, 256


def setup_inputs():
    n = np.random.standard_normal
    idx = np.random.permutation(T)[:J]
    idx2 = np.random.permutation(T)[:J]
    fk = mx_kscale(K)
    fr = mx_kscale(R)
    tabp = pack_weight(n((K, T)) / fk[:, None], "e2m1")
    dtabp = pack_weight(n((K, T)) / fk[:, None], "e2m1")
    tab2p = pack_weight(n((K, T)) / fk[:, None], "e2m1")
    dtab2p = pack_weight(n((K, T)) / fk[:, None], "e2m1")
    return {
        "tab_words": tabp[0],
        "tab_scales": tabp[1],
        "dtab_words": dtabp[0],
        "dtab_scales": dtabp[1],
        "w1": (n((K, R)) * 1 / np.sqrt(K) * fk[:, None]).astype(np.float32),
        "tab2_words": tab2p[0],
        "tab2_scales": tab2p[1],
        "dtab2_words": dtab2p[0],
        "dtab2_scales": dtab2p[1],
        "w2": (n((K, R)) * 1 / np.sqrt(K) * fk[:, None]).astype(np.float32),
        "bias": (np.random.uniform(-0.5, 0.5, (R, 1))).astype(np.float32),
        "rs": (np.random.uniform(0.5, 2.0, (R, 1)) * fr[:, None]).astype(np.float32),
        "wor": (n((R, F)) * 1 / np.sqrt(R) / fr[:, None]).astype(np.float32),
        "res": (n((F, J)) * 0.5).astype(np.float32),
        "offs": striped(idx),
        "offs2": striped(idx2),
    }


def reference(tab_words, tab_scales, dtab_words, dtab_scales, w1, tab2_words, tab2_scales, dtab2_words, dtab2_scales, w2, bias, rs, wor, res, offs, offs2):
    idx = unstriped(offs)
    idx2 = unstriped(offs2)
    tabu = unpack_weight(tab_words, tab_scales, "e2m1")
    dtabu = unpack_weight(dtab_words, dtab_scales, "e2m1")
    tab2u = unpack_weight(tab2_words, tab2_scales, "e2m1")
    dtab2u = unpack_weight(dtab2_words, dtab2_scales, "e2m1")
    w1q = mxq(f64(w1), 0, "e4m3")
    tabidxg = tabu[:, idx]
    a = w1q.T @ tabidxg
    dtabidxg = dtabu[:, idx]
    ta = w1q.T @ dtabidxg
    w2q = mxq(f64(w2), 0, "e4m3")
    tab2idx2g = tab2u[:, idx2]
    b = w2q.T @ tab2idx2g
    dtab2idx2g = dtab2u[:, idx2]
    tb = w2q.T @ dtab2idx2g
    h1 = np.tanh(a)
    gt = sigmoid(b + f64(bias))
    th1 = ta * (1.0 - np.square(h1))
    tgt = tb * gt * (1.0 - gt)
    tu1 = th1 * gt + tgt * h1
    fo1 = tu1 * f64(rs)
    worq = mxq(f64(wor), 0, "e4m3")
    fo1q = mxq(fo1, 0, "e4m3")
    yo = worq.T @ fo1q
    y = yo + f64(res)
    words, scales = planes(y)
    return y, words, scales

@@ -1,0 +1,242 @@
+from contextlib import ExitStack
+
+import concourse.mybir as mybir
+
+K, R, F, T, J = 512, 512, 512, 2048, 256
+FLOPS = 2 * (4 * K * R * J + R * F * J)
+
+F32 = mybir.dt.float32
+BF16 = mybir.dt.bfloat16
+I32 = mybir.dt.int32
+U32 = mybir.dt.uint32
+U16 = mybir.dt.uint16
+U8 = mybir.dt.uint8
+FP8X4 = mybir.dt.float8_e4m3fn_x4
+FP4X4 = mybir.dt.float4_e2m1fn_x4
+ALU = mybir.AluOpType
+ACT = mybir.ActivationFunctionType
+
+P = 128
+PACK = 4
+HALF = J // 2
+
+
+def tile_attend_tctwotables_o_pl_kernel(
+    tc, tab_words, tab_scales, dtab_words, dtab_scales, w1, tab2_words, tab2_scales, dtab2_words, dtab2_scales,
+    w2, bias, rs, wor, res, offs, offs2, out_0, out_1, out_2,
+):
+    nc = tc.nc
+    with ExitStack() as ctx:
+        sb = ctx.enter_context(tc.tile_pool(name="sb", bufs=1))
+        psum = ctx.enter_context(tc.psum_pool(name="psum", bufs=1))
+
+        def load_list(src, name):
+            t = sb.tile([P, J // 16], U16, name=name)
+            nc.sync.dma_start(t[:], src)
+            return t
+
+        def zeroed_scale_window(name, engine):
+            t = sb.tile([P, T], U8, name=name, align_bytes=64)
+            engine.memset(t[:].bitcast(I32), 0)
+            return t
+
+        def load_scales(t, src):
+            nc.scalar.dma_start(out=t[0:P:8, :].bitcast(I32), in_=src[0].bitcast(I32))
+
+        def load_words(src, name, tag):
+            t = sb.tile([P, T], U16, name=name, tag=tag, align_bytes=64)
+            nc.sync.dma_start(out=t[:].bitcast(I32), in_=src[0].bitcast(I32))
+            return t
+
+        def load_weight_cols(w, c0, c1, name, tag):
+            t = sb.tile([P, PACK, c1 - c0], F32, name=name, tag=tag, align_bytes=64)
+            nc.sync.dma_start(out=t[:], in_=w.rearrange("(p j) c -> p j c", j=PACK)[:, :, c0:c1])
+            return t
+
+        def load_by_row(v, name):
+            t = sb.tile([P, PACK], F32, name=name)
+            nc.gpsimd.dma_start(out=t[:], in_=v.rearrange("(p t) o -> p (t o)", t=PACK))
+            return t
+
+        def deal(copy, dealt, raw, m0, r0, count):
+            copy(
+                out=dealt[:, :, m0 : m0 + count, :].rearrange("p t m j -> p m j t"),
+                in_=raw[:, :, PACK * r0 : PACK * (r0 + count)].rearrange("p j (m t) -> p m j t", t=PACK),
+            )
+
+        def quantize_weight(dealt, name):
+            codes = sb.tile([P, 512], U32, name=name + "_codes", align_bytes=64)
+            scales = sb.tile([P, 512], U8, name=name + "_scales", align_bytes=64)
+            nc.vector.quantize_mx(
+                out=codes[:].bitcast(FP8X4), scales=scales[:], in_=dealt[:].rearrange("p t m j -> p (t m j)")
+            )
+            return codes, scales
+
+        def gather_words(window, lst, name):
+            g = sb.tile([P, J], U16, name=name, tag=name, align_bytes=64)
+            nc.vector.tensor_copy(g[:], window[:].indirect(lst[:]))
+            return g
+
+        def gather_scale_pair(win_a, win_b, lst, queue, name):
+            g = sb.tile([P, 2 * J], U8, name=name + "_gathered", align_bytes=64)
+            nc.vector.tensor_copy(g[:, 0:J], win_a[:].indirect(lst[:]))
+            nc.vector.tensor_copy(g[:, J : 2 * J], win_b[:].indirect(lst[:]))
+            plane = sb.tile([P, 2 * J], U8, name=name + "_plane", align_bytes=64)
+            nc.vector.tensor_copy(plane[:].bitcast(I32), g[:].bitcast(I32))
+            for r in range(1, 4):
+                queue.dma_start(out=plane[r:P:32, :].bitcast(I32), in_=g[8 * r : P : 32, :].bitcast(I32))
+            return plane
+
+        def layer(codes, scales, words, plane_cols, tag):
+            banks = []
+            for u in range(2):
+                bank = psum.tile([P, 2, J], F32, name=tag + str(u), tag=tag + str(u))
+                for e in range(2):
+                    cols = slice((2 * u + e) * P, (2 * u + e + 1) * P)
+                    nc.tensor.matmul_mx(
+                        out=bank[:, e, :], lhsT=codes[:, cols].bitcast(FP8X4), lhsT_scale=scales[:, cols],
+                        rhs=words[:].bitcast(FP4X4), rhs_scale=plane_cols, start=True, stop=True,
+                    )
+                banks.append(bank)
+            return banks
+
+        windows = []
+        for name, src, engine in (
+            ("tab2_s", tab2_scales, nc.vector), ("dtab2_s", dtab2_scales, nc.vector),
+            ("tab_s", tab_scales, nc.gpsimd), ("dtab_s", dtab_scales, nc.gpsimd),
+        ):
+            win = zeroed_scale_window(name, engine)
+            load_scales(win, src)
+            windows.append(win)
+        list2 = load_list(offs2, "list2")
+        w2_lo = load_weight_cols(w2, 0, 256, "w2_lo", "raw_lo")
+        list1 = load_list(offs, "list1")
+        w2_hi = load_weight_cols(w2, 256, 512, "w2_hi", "raw_hi")
+        tab2_w = load_words(tab2_words, "tab2_w", "words")
+        dtab2_w = load_words(dtab2_words, "dtab2_w", "dwords")
+        bias_t = load_by_row(bias, "bias_t")
+        rs_t = load_by_row(rs, "rs_t")
+
+        w2_dealt = sb.tile([P, PACK, P, PACK], BF16, name="w2_dealt", align_bytes=64)
+        deal(nc.scalar.copy, w2_dealt, w2_lo, 0, 0, 64)
+        deal(nc.scalar.copy, w2_dealt, w2_hi, 64, 0, 64)
+        w1_lo = load_weight_cols(w1, 0, 256, "w1_lo", "raw_lo")
+        w1_hi = load_weight_cols(w1, 256, 512, "w1_hi", "raw_hi")
+        plane2 = gather_scale_pair(windows[0], windows[1], list2, nc.scalar, "s2")
+        plane1 = gather_scale_pair(windows[2], windows[3], list1, nc.scalar, "s1")
+        tab2_g = gather_words(tab2_w, list2, "tab2_g")
+        w2_codes, w2_scales = quantize_weight(w2_dealt, "w2")
+        dtab2_g = gather_words(dtab2_w, list2, "dtab2_g")
+        tab_w = load_words(tab_words, "tab_w", "words")
+        dtab_w = load_words(dtab_words, "dtab_w", "dwords")
+        b_banks = layer(w2_codes, w2_scales, tab2_g, plane2[:, 0:J], "b")
+        tb_banks = layer(w2_codes, w2_scales, dtab2_g, plane2[:, J : 2 * J], "tb")
+
+        gt = sb.tile([P, PACK, J], F32, name="gt", align_bytes=64)
+        for t in range(PACK):
+            nc.scalar.activation(
+                out=gt[:, t, :], in_=b_banks[t // 2][:, t % 2, :], func=ACT.Sigmoid, bias=bias_t[:, t : t + 1]
+            )
+        neg_rs = sb.tile([P, PACK], F32, name="neg_rs")
+        nc.gpsimd.tensor_scalar(neg_rs[:], rs_t[:], -1.0, 0.0, ALU.mult, ALU.add)
+
+        w1_dealt = sb.tile([P, PACK, P, PACK], BF16, name="w1_dealt", tag="w1_dealt", align_bytes=64)
+        deal(nc.vector.tensor_copy, w1_dealt, w1_lo, 0, 0, 64)
+        q = sb.tile([P, PACK, J], F32, name="q", align_bytes=64)
+        for u in range(2):
+            nc.vector.scalar_tensor_tensor(
+                out=q[:, 2 * u : 2 * u + 2, :], in0=gt[:, 2 * u : 2 * u + 2, :], scalar=1.0, in1=tb_banks[u][:],
+                op0=ALU.subtract, op1=ALU.mult,
+            )
+        deal(nc.scalar.copy, w1_dealt, w1_hi, 64, 0, 32)
+        deal(nc.vector.tensor_copy, w1_dealt, w1_hi, 96, 32, 32)
+
+        wor_lo = load_weight_cols(wor, 0, 256, "wor_lo", "raw_lo")
+        wor_hi = load_weight_cols(wor, 256, 512, "wor_hi", "raw_hi")
+
+        tab_g = gather_words(tab_w, list1, "tab_g")
+        w1_codes, w1_scales = quantize_weight(w1_dealt, "w1")
+        res_t = sb.tile([P, PACK, J], F32, name="res_t", tag="w1_dealt", align_bytes=64)
+        nc.sync.dma_start(out=res_t[:], in_=res.rearrange("(p t) j -> p t j", t=PACK))
+        dtab_g = gather_words(dtab_w, list1, "dtab_g")
+        a_banks = layer(w1_codes, w1_scales, tab_g, plane1[:, 0:J], "a")
+        ta_banks = layer(w1_codes, w1_scales, dtab_g, plane1[:, J : 2 * J], "ta")
+
+        h = sb.tile([P, PACK, J], F32, name="h", align_bytes=64)
+        hsq = sb.tile([P, PACK, J], F32, name="hsq", align_bytes=64)
+        for u in range(2):
+            nc.scalar.activation(out=h[:, 2 * u : 2 * u + 2, :], in_=a_banks[u][:], func=ACT.Tanh)
+        for u in range(2):
+            nc.scalar.activation(out=hsq[:, 2 * u : 2 * u + 2, :], in_=h[:, 2 * u : 2 * u + 2, :], func=ACT.Square)
+        wor_dealt = sb.tile([P, PACK, P, PACK], BF16, name="wor_dealt", tag="tab_g", align_bytes=64)
+        deal(nc.scalar.copy, wor_dealt, wor_lo, 0, 0, 64)
+        deal(nc.scalar.copy, wor_dealt, wor_hi, 64, 0, 64)
+
+        q2 = sb.tile([P, PACK, J], F32, name="q2", align_bytes=64)
+        for t in range(PACK):
+            nc.vector.scalar_tensor_tensor(
+                out=q2[:, t, :], in0=q[:, t, :], scalar=neg_rs[:, t : t + 1], in1=h[:, t, :], op0=ALU.mult, op1=ALU.mult
+            )
+        pt = sb.tile([P, PACK, J], F32, name="pt", align_bytes=64)
+        for u in range(2):
+            nc.vector.scalar_tensor_tensor(
+                out=pt[:, 2 * u : 2 * u + 2, :], in0=hsq[:, 2 * u : 2 * u + 2, :], scalar=1.0, in1=ta_banks[u][:],
+                op0=ALU.subtract, op1=ALU.mult,
+            )
+        s = sb.tile([P, PACK, J], F32, name="s", align_bytes=64)
+        for t in range(PACK):
+            nc.vector.scalar_tensor_tensor(
+                out=s[:, t, :], in0=pt[:, t, :], scalar=neg_rs[:, t : t + 1], in1=q2[:, t, :], op0=ALU.mult, op1=ALU.add
+            )
+        wor_codes, wor_scales = quantize_weight(wor_dealt, "wor")
+
+        def by_lines(x):
+            return x.rearrange("p t (c i) -> p c t i", i=4)
+
+        def woven(x):
+            return x.rearrange("p (c i) t -> p c t i", i=4)
+
+        fo = []
+        for u in range(2):
+            cols = slice(u * HALF, (u + 1) * HALF)
+            fo_u = sb.tile([P, HALF, PACK], BF16, name="fo" + str(u), align_bytes=64)
+            nc.vector.tensor_tensor(out=woven(fo_u[:]), in0=by_lines(s[:, :, cols]), in1=by_lines(gt[:, :, cols]), op=ALU.mult)
+            fo.append(fo_u)
+        yo = []
+        for u in range(2):
+            codes = sb.tile([P, HALF], U32, name="fo_codes" + str(u), align_bytes=64)
+            scales = sb.tile([P, HALF], U8, name="fo_scales" + str(u), align_bytes=64)
+            nc.vector.quantize_mx(out=codes[:].bitcast(FP8X4), scales=scales[:], in_=fo[u][:].rearrange("p c t -> p (c t)"))
+            bank = psum.tile([P, PACK, HALF], F32, name="yo" + str(u), tag="b" + str(u))
+            for t in range(PACK):
+                cols = slice(t * P, (t + 1) * P)
+                nc.tensor.matmul_mx(
+                    out=bank[:, t, :], lhsT=wor_codes[:, cols].bitcast(FP8X4), lhsT_scale=wor_scales[:, cols],
+                    rhs=codes[:].bitcast(FP8X4), rhs_scale=scales[:], start=True, stop=True,
+                )
+            yo.append(bank)
+
+        y_codes = sb.tile([P, J], U32, name="y_codes", align_bytes=64)
+        y_scales = sb.tile([P, J], U8, name="y_scales", align_bytes=64)
+        out_rows = out_0.rearrange("(p t) j -> p t j", t=PACK)
+        out_words = out_1[0].rearrange("p c t -> p (c t)").bitcast(I32)
+        y_woven = []
+        for u in range(2):
+            cols = slice(u * HALF, (u + 1) * HALF)
+            y = sb.tile([P, PACK, HALF], F32, name="y" + str(u), align_bytes=64)
+            nc.vector.tensor_tensor(out=y[:], in0=yo[u][:], in1=res_t[:, :, cols], op=ALU.add)
+            nc.sync.dma_start(out=out_rows[:, :, cols], in_=y[:])
+            yw = sb.tile([P, HALF, PACK], BF16, name="yw" + str(u), align_bytes=64)
+            nc.scalar.copy(out=woven(yw[:]), in_=by_lines(y[:]))
+            y_woven.append(yw)
+        for u in range(2):
+            cols = slice(u * HALF, (u + 1) * HALF)
+            nc.vector.quantize_mx(
+                out=y_codes[:, cols].bitcast(FP8X4), scales=y_scales[:, cols], in_=y_woven[u][:].rearrange("p c t -> p (c t)")
+            )
+            nc.sync.dma_start(out=out_words[:, cols], in_=y_codes[:, cols].bitcast(I32))
+        for quad in range(4):
+            queue = nc.sync if quad % 2 == 0 else nc.scalar
+            queue.dma_start(
+                out=out_2[0, 4 * quad : 4 * quad + 4, :].bitcast(I32), in_=y_scales[32 * quad : 32 * quad + 4, :].bitcast(I32)
+            )

@@ -35,33 +35,34 @@ def tile_attend_tctwotables_o_pl_kernel(
             nc.sync.dma_start(t[:], src)
             return t
 
-        def zeroed_scale_window(name, engine):
-            t = sb.tile([P, T], U8, name=name, align_bytes=64)
-            engine.memset(t[:].bitcast(I32), 0)
+        def load_scales(src, first, name):
+            t = sb.tile([P, T], U8, name=name, tag=name, align_bytes=64)
+            nc.sync.dma_start(out=t[first : first + 16, :].bitcast(I32), in_=src[0].bitcast(I32))
             return t
 
-        def load_scales(t, src):
-            nc.scalar.dma_start(out=t[0:P:8, :].bitcast(I32), in_=src[0].bitcast(I32))
+        def zero_other_rows(t, spans, engine):
+            for lo, hi in spans:
+                engine.memset(t[lo:hi, :].bitcast(I32), 0)
 
         def load_words(src, name, tag):
             t = sb.tile([P, T], U16, name=name, tag=tag, align_bytes=64)
             nc.sync.dma_start(out=t[:].bitcast(I32), in_=src[0].bitcast(I32))
             return t
 
-        def load_weight_cols(w, c0, c1, name, tag):
-            t = sb.tile([P, PACK, c1 - c0], F32, name=name, tag=tag, align_bytes=64)
-            nc.sync.dma_start(out=t[:], in_=w.rearrange("(p j) c -> p j c", j=PACK)[:, :, c0:c1])
+        def load_weight(w, name, tag):
+            t = sb.tile([P, PACK, 512], F32, name=name, tag=tag, align_bytes=64)
+            nc.sync.dma_start(out=t[:], in_=w.rearrange("(p j) c -> p j c", j=PACK))
             return t
 
         def load_by_row(v, name):
-            t = sb.tile([P, PACK], F32, name=name)
+            t = sb.tile([P, PACK], F32, name=name, tag=name, align_bytes=64)
             nc.gpsimd.dma_start(out=t[:], in_=v.rearrange("(p t) o -> p (t o)", t=PACK))
             return t
 
-        def deal(copy, dealt, raw, m0, r0, count):
+        def deal(copy, dealt, raw, m0, count):
             copy(
                 out=dealt[:, :, m0 : m0 + count, :].rearrange("p t m j -> p m j t"),
-                in_=raw[:, :, PACK * r0 : PACK * (r0 + count)].rearrange("p j (m t) -> p m j t", t=PACK),
+                in_=raw[:, :, PACK * m0 : PACK * (m0 + count)].rearrange("p j (m t) -> p m j t", t=PACK),
             )
 
         def quantize_weight(dealt, name):
@@ -77,14 +78,17 @@ def tile_attend_tctwotables_o_pl_kernel(
             nc.vector.tensor_copy(g[:], window[:].indirect(lst[:]))
             return g
 
-        def gather_scale_pair(win_a, win_b, lst, queue, name):
+        def gather_scale_pair(win_a, win_b, first, lst, queue, name):
             g = sb.tile([P, 2 * J], U8, name=name + "_gathered", align_bytes=64)
             nc.vector.tensor_copy(g[:, 0:J], win_a[:].indirect(lst[:]))
             nc.vector.tensor_copy(g[:, J : 2 * J], win_b[:].indirect(lst[:]))
             plane = sb.tile([P, 2 * J], U8, name=name + "_plane", align_bytes=64)
-            nc.vector.tensor_copy(plane[:].bitcast(I32), g[:].bitcast(I32))
-            for r in range(1, 4):
-                queue.dma_start(out=plane[r:P:32, :].bitcast(I32), in_=g[8 * r : P : 32, :].bitcast(I32))
+            nc.gpsimd.memset(plane[:].bitcast(I32), 0)
+            for quad in range(4):
+                queue.dma_start(
+                    out=plane[32 * quad : 32 * quad + 4, :].bitcast(I32),
+                    in_=g[first + 4 * quad : first + 4 * quad + 4, :].bitcast(I32),
+                )
             return plane
 
         def layer(codes, scales, words, plane_cols, tag):
@@ -100,32 +104,35 @@ def tile_attend_tctwotables_o_pl_kernel(
                 banks.append(bank)
             return banks
 
-        windows = []
-        for name, src, engine in (
-            ("tab2_s", tab2_scales, nc.vector), ("dtab2_s", dtab2_scales, nc.vector),
-            ("tab_s", tab_scales, nc.gpsimd), ("dtab_s", dtab_scales, nc.gpsimd),
-        ):
-            win = zeroed_scale_window(name, engine)
-            load_scales(win, src)
-            windows.append(win)
+        warm_in = sb.tile([P, 1], F32, name="warm_in")
+        warm_out = sb.tile([P, 1], F32, name="warm_out")
+        nc.gpsimd.memset(warm_in[:], 0.0)
+        nc.scalar.activation(out=warm_out[:], in_=warm_in[:], func=ACT.Sigmoid)
+
         list2 = load_list(offs2, "list2")
-        w2_lo = load_weight_cols(w2, 0, 256, "w2_lo", "raw_lo")
+        tab2_s = load_scales(tab2_scales, 112, "tab2_s")
+        dtab2_s = load_scales(dtab2_scales, 112, "dtab2_s")
         list1 = load_list(offs, "list1")
-        w2_hi = load_weight_cols(w2, 256, 512, "w2_hi", "raw_hi")
+        tab_s = load_scales(tab_scales, 48, "tab_s")
+        dtab_s = load_scales(dtab_scales, 48, "dtab_s")
+        zero_other_rows(tab2_s, ((0, 112),), nc.vector)
+        zero_other_rows(dtab2_s, ((0, 112),), nc.vector)
+        zero_other_rows(tab_s, ((0, 48), (64, P)), nc.vector)
+        zero_other_rows(dtab_s, ((0, 48), (64, P)), nc.gpsimd)
+        w2_raw = load_weight(w2, "w2_raw", "w2_raw")
         tab2_w = load_words(tab2_words, "tab2_w", "words")
         dtab2_w = load_words(dtab2_words, "dtab2_w", "dwords")
         bias_t = load_by_row(bias, "bias_t")
         rs_t = load_by_row(rs, "rs_t")
 
-        w2_dealt = sb.tile([P, PACK, P, PACK], BF16, name="w2_dealt", align_bytes=64)
-        deal(nc.scalar.copy, w2_dealt, w2_lo, 0, 0, 64)
-        deal(nc.scalar.copy, w2_dealt, w2_hi, 64, 0, 64)
-        w1_lo = load_weight_cols(w1, 0, 256, "w1_lo", "raw_lo")
-        w1_hi = load_weight_cols(w1, 256, 512, "w1_hi", "raw_hi")
-        plane2 = gather_scale_pair(windows[0], windows[1], list2, nc.scalar, "s2")
-        plane1 = gather_scale_pair(windows[2], windows[3], list1, nc.scalar, "s1")
-        tab2_g = gather_words(tab2_w, list2, "tab2_g")
+        plane2 = gather_scale_pair(tab2_s, dtab2_s, 112, list2, nc.scalar, "s2")
+        w2_dealt = sb.tile([P, PACK, P, PACK], BF16, name="w2_dealt", tag="dtab2_s", align_bytes=64)
+        deal(nc.scalar.copy, w2_dealt, w2_raw, 0, 64)
+        plane1 = gather_scale_pair(tab_s, dtab_s, 48, list1, nc.sync, "s1")
+        w1_raw = load_weight(w1, "w1_raw", "dtab_s")
+        deal(nc.vector.tensor_copy, w2_dealt, w2_raw, 64, 64)
         w2_codes, w2_scales = quantize_weight(w2_dealt, "w2")
+        tab2_g = gather_words(tab2_w, list2, "tab2_g")
         dtab2_g = gather_words(dtab2_w, list2, "dtab2_g")
         tab_w = load_words(tab_words, "tab_w", "words")
         dtab_w = load_words(dtab_words, "dtab_w", "dwords")
@@ -140,25 +147,26 @@ def tile_attend_tctwotables_o_pl_kernel(
         neg_rs = sb.tile([P, PACK], F32, name="neg_rs")
         nc.gpsimd.tensor_scalar(neg_rs[:], rs_t[:], -1.0, 0.0, ALU.mult, ALU.add)
 
+        wor_raw = load_weight(wor, "wor_raw", "dtab2_g")
         w1_dealt = sb.tile([P, PACK, P, PACK], BF16, name="w1_dealt", tag="w1_dealt", align_bytes=64)
-        deal(nc.vector.tensor_copy, w1_dealt, w1_lo, 0, 0, 64)
+        deal(nc.scalar.copy, w1_dealt, w1_raw, 0, 40)
+        deal(nc.vector.tensor_copy, w1_dealt, w1_raw, 40, 88)
+
+        w1_codes, w1_scales = quantize_weight(w1_dealt, "w1")
+        tab_g = gather_words(tab_w, list1, "tab_g")
+        res_t = sb.tile([P, PACK, J], F32, name="res_t", tag="w1_dealt", align_bytes=64)
+        nc.sync.dma_start(out=res_t[:], in_=res.rearrange("(p t) j -> p t j", t=PACK))
         q = sb.tile([P, PACK, J], F32, name="q", align_bytes=64)
-        for u in range(2):
+
+        def gate_slope(u):
             nc.vector.scalar_tensor_tensor(
                 out=q[:, 2 * u : 2 * u + 2, :], in0=gt[:, 2 * u : 2 * u + 2, :], scalar=1.0, in1=tb_banks[u][:],
                 op0=ALU.subtract, op1=ALU.mult,
             )
-        deal(nc.scalar.copy, w1_dealt, w1_hi, 64, 0, 32)
-        deal(nc.vector.tensor_copy, w1_dealt, w1_hi, 96, 32, 32)
 
-        wor_lo = load_weight_cols(wor, 0, 256, "wor_lo", "raw_lo")
-        wor_hi = load_weight_cols(wor, 256, 512, "wor_hi", "raw_hi")
-
-        tab_g = gather_words(tab_w, list1, "tab_g")
-        w1_codes, w1_scales = quantize_weight(w1_dealt, "w1")
-        res_t = sb.tile([P, PACK, J], F32, name="res_t", tag="w1_dealt", align_bytes=64)
-        nc.sync.dma_start(out=res_t[:], in_=res.rearrange("(p t) j -> p t j", t=PACK))
+        gate_slope(0)
         dtab_g = gather_words(dtab_w, list1, "dtab_g")
+        gate_slope(1)
         a_banks = layer(w1_codes, w1_scales, tab_g, plane1[:, 0:J], "a")
         ta_banks = layer(w1_codes, w1_scales, dtab_g, plane1[:, J : 2 * J], "ta")
 
@@ -169,8 +177,7 @@ def tile_attend_tctwotables_o_pl_kernel(
         for u in range(2):
             nc.scalar.activation(out=hsq[:, 2 * u : 2 * u + 2, :], in_=h[:, 2 * u : 2 * u + 2, :], func=ACT.Square)
         wor_dealt = sb.tile([P, PACK, P, PACK], BF16, name="wor_dealt", tag="tab_g", align_bytes=64)
-        deal(nc.scalar.copy, wor_dealt, wor_lo, 0, 0, 64)
-        deal(nc.scalar.copy, wor_dealt, wor_hi, 64, 0, 64)
+        deal(nc.scalar.copy, wor_dealt, wor_raw, 0, P)
 
         q2 = sb.tile([P, PACK, J], F32, name="q2", align_bytes=64)
         for t in range(PACK):
@@ -188,7 +195,6 @@ def tile_attend_tctwotables_o_pl_kernel(
             nc.vector.scalar_tensor_tensor(
                 out=s[:, t, :], in0=pt[:, t, :], scalar=neg_rs[:, t : t + 1], in1=q2[:, t, :], op0=ALU.mult, op1=ALU.add
             )
-        wor_codes, wor_scales = quantize_weight(wor_dealt, "wor")
 
         def by_lines(x):
             return x.rearrange("p t (c i) -> p c t i", i=4)
@@ -196,17 +202,16 @@ def tile_attend_tctwotables_o_pl_kernel(
         def woven(x):
             return x.rearrange("p (c i) t -> p c t i", i=4)
 
-        fo = []
-        for u in range(2):
+        def weigh(u):
             cols = slice(u * HALF, (u + 1) * HALF)
             fo_u = sb.tile([P, HALF, PACK], BF16, name="fo" + str(u), align_bytes=64)
             nc.vector.tensor_tensor(out=woven(fo_u[:]), in0=by_lines(s[:, :, cols]), in1=by_lines(gt[:, :, cols]), op=ALU.mult)
-            fo.append(fo_u)
-        yo = []
-        for u in range(2):
+            return fo_u
+
+        def last_layer(u, fo_u):
             codes = sb.tile([P, HALF], U32, name="fo_codes" + str(u), align_bytes=64)
             scales = sb.tile([P, HALF], U8, name="fo_scales" + str(u), align_bytes=64)
-            nc.vector.quantize_mx(out=codes[:].bitcast(FP8X4), scales=scales[:], in_=fo[u][:].rearrange("p c t -> p (c t)"))
+            nc.vector.quantize_mx(out=codes[:].bitcast(FP8X4), scales=scales[:], in_=fo_u[:].rearrange("p c t -> p (c t)"))
             bank = psum.tile([P, PACK, HALF], F32, name="yo" + str(u), tag="b" + str(u))
             for t in range(PACK):
                 cols = slice(t * P, (t + 1) * P)
@@ -214,7 +219,12 @@ def tile_attend_tctwotables_o_pl_kernel(
                     out=bank[:, t, :], lhsT=wor_codes[:, cols].bitcast(FP8X4), lhsT_scale=wor_scales[:, cols],
                     rhs=codes[:].bitcast(FP8X4), rhs_scale=scales[:], start=True, stop=True,
                 )
-            yo.append(bank)
+            return bank
+
+        fo0 = weigh(0)
+        wor_codes, wor_scales = quantize_weight(wor_dealt, "wor")
+        yo = [last_layer(0, fo0)]
+        yo.append(last_layer(1, weigh(1)))
 
         y_codes = sb.tile([P, J], U32, name="y_codes", align_bytes=64)
         y_scales = sb.tile([P, J], U8, name="y_scales", align_bytes=64)

@@ -18,7 +18,11 @@ ACT = mybir.ActivationFunctionType
 
 P = 128
 PACK = 4
+WIDTH = 512
+BLOCKS = 16
 HALF = J // 2
+GATE_ROWS, TANH_ROWS = 112, 48
+SCALAR_SHARE = 40
 
 
 def tile_attend_tctwotables_o_pl_kernel(
@@ -31,33 +35,32 @@ def tile_attend_tctwotables_o_pl_kernel(
         psum = ctx.enter_context(tc.psum_pool(name="psum", bufs=1))
 
         def load_list(src, name):
-            t = sb.tile([P, J // 16], U16, name=name)
-            nc.sync.dma_start(t[:], src)
-            return t
+            lst = sb.tile([P, J // 16], U16, name=name)
+            nc.sync.dma_start(lst[:], src)
+            return lst
 
-        def load_scales(src, first, name):
-            t = sb.tile([P, T], U8, name=name, tag=name, align_bytes=64)
-            nc.sync.dma_start(out=t[first : first + 16, :].bitcast(I32), in_=src[0].bitcast(I32))
-            return t
-
-        def zero_other_rows(t, spans, engine):
-            for lo, hi in spans:
-                engine.memset(t[lo:hi, :].bitcast(I32), 0)
+        def load_scales(src, first, queue, engine, name):
+            window = sb.tile([P, T], U8, name=name, tag=name, align_bytes=64)
+            queue.dma_start(out=window[first : first + BLOCKS, :].bitcast(I32), in_=src[0].bitcast(I32))
+            engine.memset(window[0:first, :].bitcast(I32), 0)
+            if first + BLOCKS < P:
+                engine.memset(window[first + BLOCKS : P, :].bitcast(I32), 0)
+            return window
 
         def load_words(src, name, tag):
-            t = sb.tile([P, T], U16, name=name, tag=tag, align_bytes=64)
-            nc.sync.dma_start(out=t[:].bitcast(I32), in_=src[0].bitcast(I32))
-            return t
+            window = sb.tile([P, T], U16, name=name, tag=tag, align_bytes=64)
+            nc.sync.dma_start(out=window[:].bitcast(I32), in_=src[0].bitcast(I32))
+            return window
 
         def load_weight(w, name, tag):
-            t = sb.tile([P, PACK, 512], F32, name=name, tag=tag, align_bytes=64)
-            nc.sync.dma_start(out=t[:], in_=w.rearrange("(p j) c -> p j c", j=PACK))
-            return t
+            raw = sb.tile([P, PACK, WIDTH], F32, name=name, tag=tag, align_bytes=64)
+            nc.sync.dma_start(out=raw[:], in_=w.rearrange("(p j) c -> p j c", j=PACK))
+            return raw
 
-        def load_by_row(v, name):
-            t = sb.tile([P, PACK], F32, name=name, tag=name, align_bytes=64)
-            nc.gpsimd.dma_start(out=t[:], in_=v.rearrange("(p t) o -> p (t o)", t=PACK))
-            return t
+        def load_by_row(vec, name):
+            by_row = sb.tile([P, PACK], F32, name=name, tag=name, align_bytes=64)
+            nc.gpsimd.dma_start(out=by_row[:], in_=vec.rearrange("(p t) o -> p (t o)", t=PACK))
+            return by_row
 
         def deal(copy, dealt, raw, m0, count):
             copy(
@@ -66,78 +69,81 @@ def tile_attend_tctwotables_o_pl_kernel(
             )
 
         def quantize_weight(dealt, name):
-            codes = sb.tile([P, 512], U32, name=name + "_codes", align_bytes=64)
-            scales = sb.tile([P, 512], U8, name=name + "_scales", align_bytes=64)
+            codes = sb.tile([P, WIDTH], U32, name=name + "_codes", align_bytes=64)
+            scales = sb.tile([P, WIDTH], U8, name=name + "_scales", align_bytes=64)
             nc.vector.quantize_mx(
                 out=codes[:].bitcast(FP8X4), scales=scales[:], in_=dealt[:].rearrange("p t m j -> p (t m j)")
             )
             return codes, scales
 
-        def gather_words(window, lst, name):
-            g = sb.tile([P, J], U16, name=name, tag=name, align_bytes=64)
-            nc.vector.tensor_copy(g[:], window[:].indirect(lst[:]))
-            return g
+        def gather_words(window, lst, name, tag):
+            words = sb.tile([P, J], U16, name=name, tag=tag, align_bytes=64)
+            nc.vector.tensor_copy(words[:], window[:].indirect(lst[:]))
+            return words
 
-        def gather_scale_pair(win_a, win_b, first, lst, queue, name):
-            g = sb.tile([P, 2 * J], U8, name=name + "_gathered", align_bytes=64)
-            nc.vector.tensor_copy(g[:, 0:J], win_a[:].indirect(lst[:]))
-            nc.vector.tensor_copy(g[:, J : 2 * J], win_b[:].indirect(lst[:]))
-            plane = sb.tile([P, 2 * J], U8, name=name + "_plane", align_bytes=64)
-            nc.gpsimd.memset(plane[:].bitcast(I32), 0)
+        def gather_scales(window, tangent_window, lst, name):
+            gathered = sb.tile([P, 2 * J], U8, name=name, align_bytes=64)
+            nc.vector.tensor_copy(gathered[:, 0:J], window[:].indirect(lst[:]))
+            nc.vector.tensor_copy(gathered[:, J : 2 * J], tangent_window[:].indirect(lst[:]))
+            return gathered
+
+        def place_rows(gathered, first, engine, name, tag):
+            placed = sb.tile([P, 2 * J], U8, name=name, tag=tag, align_bytes=64)
+            engine.memset(placed[:].bitcast(I32), 0)
             for quad in range(4):
-                queue.dma_start(
-                    out=plane[32 * quad : 32 * quad + 4, :].bitcast(I32),
-                    in_=g[first + 4 * quad : first + 4 * quad + 4, :].bitcast(I32),
+                nc.sync.dma_start(
+                    out=placed[32 * quad : 32 * quad + 4, :].bitcast(I32),
+                    in_=gathered[first + 4 * quad : first + 4 * quad + 4, :].bitcast(I32),
                 )
-            return plane
+            return placed
 
-        def layer(codes, scales, words, plane_cols, tag):
+        def layer(codes, scales, words, word_scales, bank_tags):
+            per_bank = PACK // len(bank_tags)
             banks = []
-            for u in range(2):
-                bank = psum.tile([P, 2, J], F32, name=tag + str(u), tag=tag + str(u))
-                for e in range(2):
-                    cols = slice((2 * u + e) * P, (2 * u + e + 1) * P)
+            for i, tag in enumerate(bank_tags):
+                bank = psum.tile([P, per_bank, J], F32, name=tag + "_bank", tag=tag)
+                for e in range(per_bank):
+                    cols = slice((per_bank * i + e) * P, (per_bank * i + e + 1) * P)
                     nc.tensor.matmul_mx(
                         out=bank[:, e, :], lhsT=codes[:, cols].bitcast(FP8X4), lhsT_scale=scales[:, cols],
-                        rhs=words[:].bitcast(FP4X4), rhs_scale=plane_cols, start=True, stop=True,
+                        rhs=words[:].bitcast(FP4X4), rhs_scale=word_scales, start=True, stop=True,
                     )
                 banks.append(bank)
             return banks
+
+        list2 = load_list(offs2, "list2")
+        list1 = load_list(offs, "list1")
+        tab2_s = load_scales(tab2_scales, GATE_ROWS, nc.scalar, nc.vector, "tab2_s")
+        dtab2_s = load_scales(dtab2_scales, GATE_ROWS, nc.scalar, nc.vector, "dtab2_s")
+        tab_s = load_scales(tab_scales, TANH_ROWS, nc.sync, nc.vector, "tab_s")
+        dtab_s = load_scales(dtab_scales, TANH_ROWS, nc.sync, nc.gpsimd, "dtab_s")
+        tab2_w = load_words(tab2_words, "tab2_w", "words")
+        w2_raw = load_weight(w2, "w2_raw", "w2_raw")
+        dtab2_w = load_words(dtab2_words, "dtab2_w", "dwords")
 
         warm_in = sb.tile([P, 1], F32, name="warm_in")
         warm_out = sb.tile([P, 1], F32, name="warm_out")
         nc.gpsimd.memset(warm_in[:], 0.0)
         nc.scalar.activation(out=warm_out[:], in_=warm_in[:], func=ACT.Sigmoid)
 
-        list2 = load_list(offs2, "list2")
-        tab2_s = load_scales(tab2_scales, 112, "tab2_s")
-        dtab2_s = load_scales(dtab2_scales, 112, "dtab2_s")
-        list1 = load_list(offs, "list1")
-        tab_s = load_scales(tab_scales, 48, "tab_s")
-        dtab_s = load_scales(dtab_scales, 48, "dtab_s")
-        zero_other_rows(tab2_s, ((0, 112),), nc.vector)
-        zero_other_rows(dtab2_s, ((0, 112),), nc.vector)
-        zero_other_rows(tab_s, ((0, 48), (64, P)), nc.vector)
-        zero_other_rows(dtab_s, ((0, 48), (64, P)), nc.gpsimd)
-        w2_raw = load_weight(w2, "w2_raw", "w2_raw")
-        tab2_w = load_words(tab2_words, "tab2_w", "words")
-        dtab2_w = load_words(dtab2_words, "dtab2_w", "dwords")
+        gathered2 = gather_scales(tab2_s, dtab2_s, list2, "gathered2")
+        placed2 = place_rows(gathered2, GATE_ROWS, nc.gpsimd, "placed2", "placed2")
+        tab_w = load_words(tab_words, "tab_w", "dtab2_s")
         bias_t = load_by_row(bias, "bias_t")
         rs_t = load_by_row(rs, "rs_t")
+        gathered1 = gather_scales(tab_s, dtab_s, list1, "gathered1")
+        w1_raw = load_weight(w1, "w1_raw", "tab_s")
+        tab2_g = gather_words(tab2_w, list2, "tab2_g", "tab2_g")
+        placed1 = place_rows(gathered1, TANH_ROWS, nc.vector, "placed1", "words")
 
-        plane2 = gather_scale_pair(tab2_s, dtab2_s, 112, list2, nc.scalar, "s2")
-        w2_dealt = sb.tile([P, PACK, P, PACK], BF16, name="w2_dealt", tag="dtab2_s", align_bytes=64)
-        deal(nc.scalar.copy, w2_dealt, w2_raw, 0, 64)
-        plane1 = gather_scale_pair(tab_s, dtab_s, 48, list1, nc.sync, "s1")
-        w1_raw = load_weight(w1, "w1_raw", "dtab_s")
-        deal(nc.vector.tensor_copy, w2_dealt, w2_raw, 64, 64)
+        w2_dealt = sb.tile([P, PACK, P, PACK], BF16, name="w2_dealt", tag="dtab_s", align_bytes=64)
+        deal(nc.scalar.copy, w2_dealt, w2_raw, 0, SCALAR_SHARE)
+        deal(nc.vector.tensor_copy, w2_dealt, w2_raw, SCALAR_SHARE, P - SCALAR_SHARE)
         w2_codes, w2_scales = quantize_weight(w2_dealt, "w2")
-        tab2_g = gather_words(tab2_w, list2, "tab2_g")
-        dtab2_g = gather_words(dtab2_w, list2, "dtab2_g")
-        tab_w = load_words(tab_words, "tab_w", "words")
+        dtab2_g = gather_words(dtab2_w, list2, "dtab2_g", "dtab_s")
         dtab_w = load_words(dtab_words, "dtab_w", "dwords")
-        b_banks = layer(w2_codes, w2_scales, tab2_g, plane2[:, 0:J], "b")
-        tb_banks = layer(w2_codes, w2_scales, dtab2_g, plane2[:, J : 2 * J], "tb")
+        b_banks = layer(w2_codes, w2_scales, tab2_g, placed2[:, 0:J], ("p0", "p1"))
+        tb_banks = layer(w2_codes, w2_scales, dtab2_g, placed2[:, J : 2 * J], ("p2", "p3"))
 
         gt = sb.tile([P, PACK, J], F32, name="gt", align_bytes=64)
         for t in range(PACK):
@@ -147,72 +153,76 @@ def tile_attend_tctwotables_o_pl_kernel(
         neg_rs = sb.tile([P, PACK], F32, name="neg_rs")
         nc.gpsimd.tensor_scalar(neg_rs[:], rs_t[:], -1.0, 0.0, ALU.mult, ALU.add)
 
-        wor_raw = load_weight(wor, "wor_raw", "dtab2_g")
-        w1_dealt = sb.tile([P, PACK, P, PACK], BF16, name="w1_dealt", tag="w1_dealt", align_bytes=64)
-        deal(nc.scalar.copy, w1_dealt, w1_raw, 0, 40)
-        deal(nc.vector.tensor_copy, w1_dealt, w1_raw, 40, 88)
-
-        w1_codes, w1_scales = quantize_weight(w1_dealt, "w1")
-        tab_g = gather_words(tab_w, list1, "tab_g")
-        res_t = sb.tile([P, PACK, J], F32, name="res_t", tag="w1_dealt", align_bytes=64)
-        nc.sync.dma_start(out=res_t[:], in_=res.rearrange("(p t) j -> p t j", t=PACK))
-        q = sb.tile([P, PACK, J], F32, name="q", align_bytes=64)
-
-        def gate_slope(u):
+        wor_raw = load_weight(wor, "wor_raw", "dtab_s")
+        tab_g = gather_words(tab_w, list1, "tab_g", "tab_g")
+        slope = sb.tile([P, PACK, J], F32, name="slope", align_bytes=64)
+        for pair in range(2):
+            tiles = slice(2 * pair, 2 * pair + 2)
             nc.vector.scalar_tensor_tensor(
-                out=q[:, 2 * u : 2 * u + 2, :], in0=gt[:, 2 * u : 2 * u + 2, :], scalar=1.0, in1=tb_banks[u][:],
+                out=slope[:, tiles, :], in0=gt[:, tiles, :], scalar=1.0, in1=tb_banks[pair][:],
                 op0=ALU.subtract, op1=ALU.mult,
             )
 
-        gate_slope(0)
-        dtab_g = gather_words(dtab_w, list1, "dtab_g")
-        gate_slope(1)
-        a_banks = layer(w1_codes, w1_scales, tab_g, plane1[:, 0:J], "a")
-        ta_banks = layer(w1_codes, w1_scales, dtab_g, plane1[:, J : 2 * J], "ta")
+        w1_dealt = sb.tile([P, PACK, P, PACK], BF16, name="w1_dealt", tag="w1_dealt", align_bytes=64)
+        deal(nc.scalar.copy, w1_dealt, w1_raw, 0, SCALAR_SHARE)
+        deal(nc.vector.tensor_copy, w1_dealt, w1_raw, SCALAR_SHARE, P - SCALAR_SHARE)
+        w1_codes, w1_scales = quantize_weight(w1_dealt, "w1")
+        dtab_g = gather_words(dtab_w, list1, "dtab_g", "w1_dealt")
+        res_t = sb.tile([P, PACK, J], F32, name="res_t", tag="dwords", align_bytes=64)
+        nc.sync.dma_start(out=res_t[:], in_=res.rearrange("(p t) j -> p t j", t=PACK))
+        a_banks = layer(w1_codes, w1_scales, tab_g, placed1[:, 0:J], ("p4", "p5", "p0", "p1"))
+        ta_banks = layer(w1_codes, w1_scales, dtab_g, placed1[:, J : 2 * J], ("p6", "p7"))
 
         h = sb.tile([P, PACK, J], F32, name="h", align_bytes=64)
         hsq = sb.tile([P, PACK, J], F32, name="hsq", align_bytes=64)
-        for u in range(2):
-            nc.scalar.activation(out=h[:, 2 * u : 2 * u + 2, :], in_=a_banks[u][:], func=ACT.Tanh)
-        for u in range(2):
-            nc.scalar.activation(out=hsq[:, 2 * u : 2 * u + 2, :], in_=h[:, 2 * u : 2 * u + 2, :], func=ACT.Square)
+        for t in range(PACK):
+            nc.scalar.activation(out=h[:, t, :], in_=a_banks[t][:, 0, :], func=ACT.Tanh)
+        for pair in range(2):
+            tiles = slice(2 * pair, 2 * pair + 2)
+            nc.scalar.activation(out=hsq[:, tiles, :], in_=h[:, tiles, :], func=ACT.Square)
         wor_dealt = sb.tile([P, PACK, P, PACK], BF16, name="wor_dealt", tag="tab_g", align_bytes=64)
         deal(nc.scalar.copy, wor_dealt, wor_raw, 0, P)
 
-        q2 = sb.tile([P, PACK, J], F32, name="q2", align_bytes=64)
+        gate_term = sb.tile([P, PACK, J], F32, name="gate_term", align_bytes=64)
         for t in range(PACK):
             nc.vector.scalar_tensor_tensor(
-                out=q2[:, t, :], in0=q[:, t, :], scalar=neg_rs[:, t : t + 1], in1=h[:, t, :], op0=ALU.mult, op1=ALU.mult
+                out=gate_term[:, t, :], in0=slope[:, t, :], scalar=neg_rs[:, t : t + 1], in1=h[:, t, :],
+                op0=ALU.mult, op1=ALU.mult,
             )
-        pt = sb.tile([P, PACK, J], F32, name="pt", align_bytes=64)
-        for u in range(2):
+        neg_th = sb.tile([P, PACK, J], F32, name="neg_th", align_bytes=64)
+        for pair in range(2):
+            tiles = slice(2 * pair, 2 * pair + 2)
             nc.vector.scalar_tensor_tensor(
-                out=pt[:, 2 * u : 2 * u + 2, :], in0=hsq[:, 2 * u : 2 * u + 2, :], scalar=1.0, in1=ta_banks[u][:],
+                out=neg_th[:, tiles, :], in0=hsq[:, tiles, :], scalar=1.0, in1=ta_banks[pair][:],
                 op0=ALU.subtract, op1=ALU.mult,
             )
-        s = sb.tile([P, PACK, J], F32, name="s", align_bytes=64)
+        inner = sb.tile([P, PACK, J], F32, name="inner", align_bytes=64)
         for t in range(PACK):
             nc.vector.scalar_tensor_tensor(
-                out=s[:, t, :], in0=pt[:, t, :], scalar=neg_rs[:, t : t + 1], in1=q2[:, t, :], op0=ALU.mult, op1=ALU.add
+                out=inner[:, t, :], in0=neg_th[:, t, :], scalar=neg_rs[:, t : t + 1], in1=gate_term[:, t, :],
+                op0=ALU.mult, op1=ALU.add,
             )
 
-        def by_lines(x):
-            return x.rearrange("p t (c i) -> p c t i", i=4)
+        def weave(words, tiles):
+            nc.scalar.copy(
+                out=words[:].rearrange("p (c i) t -> p c t i", i=4), in_=tiles[:].rearrange("p t (c i) -> p c t i", i=4)
+            )
 
-        def woven(x):
-            return x.rearrange("p (c i) t -> p c t i", i=4)
+        def make_fo1(half):
+            cols = slice(half * HALF, (half + 1) * HALF)
+            fo_tiles = sb.tile([P, PACK, HALF], BF16, name="fo_tiles" + str(half), align_bytes=64)
+            nc.vector.tensor_tensor(out=fo_tiles[:], in0=inner[:, :, cols], in1=gt[:, :, cols], op=ALU.mult)
+            fo_words = sb.tile([P, HALF, PACK], BF16, name="fo_words" + str(half), align_bytes=64)
+            weave(fo_words, fo_tiles)
+            return fo_words
 
-        def weigh(u):
-            cols = slice(u * HALF, (u + 1) * HALF)
-            fo_u = sb.tile([P, HALF, PACK], BF16, name="fo" + str(u), align_bytes=64)
-            nc.vector.tensor_tensor(out=woven(fo_u[:]), in0=by_lines(s[:, :, cols]), in1=by_lines(gt[:, :, cols]), op=ALU.mult)
-            return fo_u
-
-        def last_layer(u, fo_u):
-            codes = sb.tile([P, HALF], U32, name="fo_codes" + str(u), align_bytes=64)
-            scales = sb.tile([P, HALF], U8, name="fo_scales" + str(u), align_bytes=64)
-            nc.vector.quantize_mx(out=codes[:].bitcast(FP8X4), scales=scales[:], in_=fo_u[:].rearrange("p c t -> p (c t)"))
-            bank = psum.tile([P, PACK, HALF], F32, name="yo" + str(u), tag="b" + str(u))
+        def last_layer(half, fo_words):
+            codes = sb.tile([P, HALF], U32, name="fo_codes" + str(half), align_bytes=64)
+            scales = sb.tile([P, HALF], U8, name="fo_scales" + str(half), align_bytes=64)
+            nc.vector.quantize_mx(
+                out=codes[:].bitcast(FP8X4), scales=scales[:], in_=fo_words[:].rearrange("p c t -> p (c t)")
+            )
+            bank = psum.tile([P, PACK, HALF], F32, name="yo" + str(half), tag="p" + str(2 + half))
             for t in range(PACK):
                 cols = slice(t * P, (t + 1) * P)
                 nc.tensor.matmul_mx(
@@ -221,32 +231,33 @@ def tile_attend_tctwotables_o_pl_kernel(
                 )
             return bank
 
-        fo0 = weigh(0)
+        fo1 = [make_fo1(0), make_fo1(1)]
         wor_codes, wor_scales = quantize_weight(wor_dealt, "wor")
-        yo = [last_layer(0, fo0)]
-        yo.append(last_layer(1, weigh(1)))
+        yo = [last_layer(0, fo1[0]), last_layer(1, fo1[1])]
 
         y_codes = sb.tile([P, J], U32, name="y_codes", align_bytes=64)
         y_scales = sb.tile([P, J], U8, name="y_scales", align_bytes=64)
         out_rows = out_0.rearrange("(p t) j -> p t j", t=PACK)
         out_words = out_1[0].rearrange("p c t -> p (c t)").bitcast(I32)
-        y_woven = []
-        for u in range(2):
-            cols = slice(u * HALF, (u + 1) * HALF)
-            y = sb.tile([P, PACK, HALF], F32, name="y" + str(u), align_bytes=64)
-            nc.vector.tensor_tensor(out=y[:], in0=yo[u][:], in1=res_t[:, :, cols], op=ALU.add)
+        y_words = []
+        for half in range(2):
+            cols = slice(half * HALF, (half + 1) * HALF)
+            woven = sb.tile([P, HALF, PACK], BF16, name="y_words" + str(half), align_bytes=64)
+            y = sb.tile([P, PACK, HALF], F32, name="y" + str(half), align_bytes=64)
+            nc.vector.tensor_tensor(out=y[:], in0=yo[half][:], in1=res_t[:, :, cols], op=ALU.add)
             nc.sync.dma_start(out=out_rows[:, :, cols], in_=y[:])
-            yw = sb.tile([P, HALF, PACK], BF16, name="yw" + str(u), align_bytes=64)
-            nc.scalar.copy(out=woven(yw[:]), in_=by_lines(y[:]))
-            y_woven.append(yw)
-        for u in range(2):
-            cols = slice(u * HALF, (u + 1) * HALF)
+            weave(woven, y)
+            y_words.append(woven)
+        for half in range(2):
+            cols = slice(half * HALF, (half + 1) * HALF)
             nc.vector.quantize_mx(
-                out=y_codes[:, cols].bitcast(FP8X4), scales=y_scales[:, cols], in_=y_woven[u][:].rearrange("p c t -> p (c t)")
+                out=y_codes[:, cols].bitcast(FP8X4), scales=y_scales[:, cols],
+                in_=y_words[half][:].rearrange("p c t -> p (c t)"),
             )
             nc.sync.dma_start(out=out_words[:, cols], in_=y_codes[:, cols].bitcast(I32))
         for quad in range(4):
             queue = nc.sync if quad % 2 == 0 else nc.scalar
             queue.dma_start(
-                out=out_2[0, 4 * quad : 4 * quad + 4, :].bitcast(I32), in_=y_scales[32 * quad : 32 * quad + 4, :].bitcast(I32)
+                out=out_2[0, 4 * quad : 4 * quad + 4, :].bitcast(I32),
+                in_=y_scales[32 * quad : 32 * quad + 4, :].bitcast(I32),
             )

from contextlib import ExitStack

import concourse.mybir as mybir

K, R, F, T, J = 512, 512, 512, 2048, 256
FLOPS = 2 * (4 * K * R * J + R * F * J)

F32 = mybir.dt.float32
BF16 = mybir.dt.bfloat16
I32 = mybir.dt.int32
U32 = mybir.dt.uint32
U16 = mybir.dt.uint16
U8 = mybir.dt.uint8
FP8X4 = mybir.dt.float8_e4m3fn_x4
FP4X4 = mybir.dt.float4_e2m1fn_x4
ALU = mybir.AluOpType
ACT = mybir.ActivationFunctionType

P = 128
PACK = 4
WIDTH = 512
BLOCKS = 16
HALF = J // 2
GATE_ROWS, TANH_ROWS = 112, 48
SCALAR_SHARE = 40


def tile_attend_tctwotables_o_pl_kernel(
    tc, tab_words, tab_scales, dtab_words, dtab_scales, w1, tab2_words, tab2_scales, dtab2_words, dtab2_scales,
    w2, bias, rs, wor, res, offs, offs2, out_0, out_1, out_2,
):
    nc = tc.nc
    with ExitStack() as ctx:
        sb = ctx.enter_context(tc.tile_pool(name="sb", bufs=1))
        psum = ctx.enter_context(tc.psum_pool(name="psum", bufs=1))

        def load_list(src, name):
            lst = sb.tile([P, J // 16], U16, name=name)
            nc.sync.dma_start(lst[:], src)
            return lst

        def load_scales(src, first, queue, engine, name):
            window = sb.tile([P, T], U8, name=name, tag=name, align_bytes=64)
            queue.dma_start(out=window[first : first + BLOCKS, :].bitcast(I32), in_=src[0].bitcast(I32))
            engine.memset(window[0:first, :].bitcast(I32), 0)
            if first + BLOCKS < P:
                engine.memset(window[first + BLOCKS : P, :].bitcast(I32), 0)
            return window

        def load_words(src, name, tag):
            window = sb.tile([P, T], U16, name=name, tag=tag, align_bytes=64)
            nc.sync.dma_start(out=window[:].bitcast(I32), in_=src[0].bitcast(I32))
            return window

        def load_weight(w, name, tag):
            raw = sb.tile([P, PACK, WIDTH], F32, name=name, tag=tag, align_bytes=64)
            nc.sync.dma_start(out=raw[:], in_=w.rearrange("(p j) c -> p j c", j=PACK))
            return raw

        def load_by_row(vec, name):
            by_row = sb.tile([P, PACK], F32, name=name, tag=name, align_bytes=64)
            nc.gpsimd.dma_start(out=by_row[:], in_=vec.rearrange("(p t) o -> p (t o)", t=PACK))
            return by_row

        def deal(copy, dealt, raw, m0, count):
            copy(
                out=dealt[:, :, m0 : m0 + count, :].rearrange("p t m j -> p m j t"),
                in_=raw[:, :, PACK * m0 : PACK * (m0 + count)].rearrange("p j (m t) -> p m j t", t=PACK),
            )

        def quantize_weight(dealt, name):
            codes = sb.tile([P, WIDTH], U32, name=name + "_codes", align_bytes=64)
            scales = sb.tile([P, WIDTH], U8, name=name + "_scales", align_bytes=64)
            nc.vector.quantize_mx(
                out=codes[:].bitcast(FP8X4), scales=scales[:], in_=dealt[:].rearrange("p t m j -> p (t m j)")
            )
            return codes, scales

        def gather_words(window, lst, name, tag):
            words = sb.tile([P, J], U16, name=name, tag=tag, align_bytes=64)
            nc.vector.tensor_copy(words[:], window[:].indirect(lst[:]))
            return words

        def gather_scales(window, tangent_window, lst, name):
            gathered = sb.tile([P, 2 * J], U8, name=name, align_bytes=64)
            nc.vector.tensor_copy(gathered[:, 0:J], window[:].indirect(lst[:]))
            nc.vector.tensor_copy(gathered[:, J : 2 * J], tangent_window[:].indirect(lst[:]))
            return gathered

        def place_rows(gathered, first, engine, name, tag):
            placed = sb.tile([P, 2 * J], U8, name=name, tag=tag, align_bytes=64)
            engine.memset(placed[:].bitcast(I32), 0)
            for quad in range(4):
                nc.sync.dma_start(
                    out=placed[32 * quad : 32 * quad + 4, :].bitcast(I32),
                    in_=gathered[first + 4 * quad : first + 4 * quad + 4, :].bitcast(I32),
                )
            return placed

        def layer(codes, scales, words, word_scales, bank_tags):
            per_bank = PACK // len(bank_tags)
            banks = []
            for i, tag in enumerate(bank_tags):
                bank = psum.tile([P, per_bank, J], F32, name=tag + "_bank", tag=tag)
                for e in range(per_bank):
                    cols = slice((per_bank * i + e) * P, (per_bank * i + e + 1) * P)
                    nc.tensor.matmul_mx(
                        out=bank[:, e, :], lhsT=codes[:, cols].bitcast(FP8X4), lhsT_scale=scales[:, cols],
                        rhs=words[:].bitcast(FP4X4), rhs_scale=word_scales, start=True, stop=True,
                    )
                banks.append(bank)
            return banks

        list2 = load_list(offs2, "list2")
        list1 = load_list(offs, "list1")
        tab2_s = load_scales(tab2_scales, GATE_ROWS, nc.scalar, nc.vector, "tab2_s")
        dtab2_s = load_scales(dtab2_scales, GATE_ROWS, nc.scalar, nc.vector, "dtab2_s")
        tab_s = load_scales(tab_scales, TANH_ROWS, nc.sync, nc.vector, "tab_s")
        dtab_s = load_scales(dtab_scales, TANH_ROWS, nc.sync, nc.gpsimd, "dtab_s")
        tab2_w = load_words(tab2_words, "tab2_w", "words")
        w2_raw = load_weight(w2, "w2_raw", "w2_raw")
        dtab2_w = load_words(dtab2_words, "dtab2_w", "dwords")

        warm_in = sb.tile([P, 1], F32, name="warm_in")
        warm_out = sb.tile([P, 1], F32, name="warm_out")
        nc.gpsimd.memset(warm_in[:], 0.0)
        nc.scalar.activation(out=warm_out[:], in_=warm_in[:], func=ACT.Sigmoid)

        gathered2 = gather_scales(tab2_s, dtab2_s, list2, "gathered2")
        placed2 = place_rows(gathered2, GATE_ROWS, nc.gpsimd, "placed2", "placed2")
        tab_w = load_words(tab_words, "tab_w", "dtab2_s")
        bias_t = load_by_row(bias, "bias_t")
        rs_t = load_by_row(rs, "rs_t")
        gathered1 = gather_scales(tab_s, dtab_s, list1, "gathered1")
        w1_raw = load_weight(w1, "w1_raw", "tab_s")
        tab2_g = gather_words(tab2_w, list2, "tab2_g", "tab2_g")
        placed1 = place_rows(gathered1, TANH_ROWS, nc.vector, "placed1", "words")

        w2_dealt = sb.tile([P, PACK, P, PACK], BF16, name="w2_dealt", tag="dtab_s", align_bytes=64)
        deal(nc.scalar.copy, w2_dealt, w2_raw, 0, SCALAR_SHARE)
        deal(nc.vector.tensor_copy, w2_dealt, w2_raw, SCALAR_SHARE, P - SCALAR_SHARE)
        w2_codes, w2_scales = quantize_weight(w2_dealt, "w2")
        dtab2_g = gather_words(dtab2_w, list2, "dtab2_g", "dtab_s")
        dtab_w = load_words(dtab_words, "dtab_w", "dwords")
        b_banks = layer(w2_codes, w2_scales, tab2_g, placed2[:, 0:J], ("p0", "p1"))
        tb_banks = layer(w2_codes, w2_scales, dtab2_g, placed2[:, J : 2 * J], ("p2", "p3"))

        gt = sb.tile([P, PACK, J], F32, name="gt", align_bytes=64)
        for t in range(PACK):
            nc.scalar.activation(
                out=gt[:, t, :], in_=b_banks[t // 2][:, t % 2, :], func=ACT.Sigmoid, bias=bias_t[:, t : t + 1]
            )
        neg_rs = sb.tile([P, PACK], F32, name="neg_rs")
        nc.gpsimd.tensor_scalar(neg_rs[:], rs_t[:], -1.0, 0.0, ALU.mult, ALU.add)

        wor_raw = load_weight(wor, "wor_raw", "dtab_s")
        tab_g = gather_words(tab_w, list1, "tab_g", "tab_g")
        slope = sb.tile([P, PACK, J], F32, name="slope", align_bytes=64)
        for pair in range(2):
            tiles = slice(2 * pair, 2 * pair + 2)
            nc.vector.scalar_tensor_tensor(
                out=slope[:, tiles, :], in0=gt[:, tiles, :], scalar=1.0, in1=tb_banks[pair][:],
                op0=ALU.subtract, op1=ALU.mult,
            )

        w1_dealt = sb.tile([P, PACK, P, PACK], BF16, name="w1_dealt", tag="w1_dealt", align_bytes=64)
        deal(nc.scalar.copy, w1_dealt, w1_raw, 0, SCALAR_SHARE)
        deal(nc.vector.tensor_copy, w1_dealt, w1_raw, SCALAR_SHARE, P - SCALAR_SHARE)
        w1_codes, w1_scales = quantize_weight(w1_dealt, "w1")
        dtab_g = gather_words(dtab_w, list1, "dtab_g", "w1_dealt")
        res_t = sb.tile([P, PACK, J], F32, name="res_t", tag="dwords", align_bytes=64)
        nc.sync.dma_start(out=res_t[:], in_=res.rearrange("(p t) j -> p t j", t=PACK))
        a_banks = layer(w1_codes, w1_scales, tab_g, placed1[:, 0:J], ("p4", "p5", "p0", "p1"))
        ta_banks = layer(w1_codes, w1_scales, dtab_g, placed1[:, J : 2 * J], ("p6", "p7"))

        h = sb.tile([P, PACK, J], F32, name="h", align_bytes=64)
        hsq = sb.tile([P, PACK, J], F32, name="hsq", align_bytes=64)
        for t in range(PACK):
            nc.scalar.activation(out=h[:, t, :], in_=a_banks[t][:, 0, :], func=ACT.Tanh)
        for pair in range(2):
            tiles = slice(2 * pair, 2 * pair + 2)
            nc.scalar.activation(out=hsq[:, tiles, :], in_=h[:, tiles, :], func=ACT.Square)
        wor_dealt = sb.tile([P, PACK, P, PACK], BF16, name="wor_dealt", tag="tab_g", align_bytes=64)
        deal(nc.scalar.copy, wor_dealt, wor_raw, 0, P)

        gate_term = sb.tile([P, PACK, J], F32, name="gate_term", align_bytes=64)
        for t in range(PACK):
            nc.vector.scalar_tensor_tensor(
                out=gate_term[:, t, :], in0=slope[:, t, :], scalar=neg_rs[:, t : t + 1], in1=h[:, t, :],
                op0=ALU.mult, op1=ALU.mult,
            )
        neg_th = sb.tile([P, PACK, J], F32, name="neg_th", align_bytes=64)
        for pair in range(2):
            tiles = slice(2 * pair, 2 * pair + 2)
            nc.vector.scalar_tensor_tensor(
                out=neg_th[:, tiles, :], in0=hsq[:, tiles, :], scalar=1.0, in1=ta_banks[pair][:],
                op0=ALU.subtract, op1=ALU.mult,
            )
        inner = sb.tile([P, PACK, J], F32, name="inner", align_bytes=64)
        for t in range(PACK):
            nc.vector.scalar_tensor_tensor(
                out=inner[:, t, :], in0=neg_th[:, t, :], scalar=neg_rs[:, t : t + 1], in1=gate_term[:, t, :],
                op0=ALU.mult, op1=ALU.add,
            )

        def weave(words, tiles):
            nc.scalar.copy(
                out=words[:].rearrange("p (c i) t -> p c t i", i=4), in_=tiles[:].rearrange("p t (c i) -> p c t i", i=4)
            )

        def make_fo1(half):
            cols = slice(half * HALF, (half + 1) * HALF)
            fo_tiles = sb.tile([P, PACK, HALF], BF16, name="fo_tiles" + str(half), align_bytes=64)
            nc.vector.tensor_tensor(out=fo_tiles[:], in0=inner[:, :, cols], in1=gt[:, :, cols], op=ALU.mult)
            fo_words = sb.tile([P, HALF, PACK], BF16, name="fo_words" + str(half), align_bytes=64)
            weave(fo_words, fo_tiles)
            return fo_words

        def last_layer(half, fo_words):
            codes = sb.tile([P, HALF], U32, name="fo_codes" + str(half), align_bytes=64)
            scales = sb.tile([P, HALF], U8, name="fo_scales" + str(half), align_bytes=64)
            nc.vector.quantize_mx(
                out=codes[:].bitcast(FP8X4), scales=scales[:], in_=fo_words[:].rearrange("p c t -> p (c t)")
            )
            bank = psum.tile([P, PACK, HALF], F32, name="yo" + str(half), tag="p" + str(2 + half))
            for t in range(PACK):
                cols = slice(t * P, (t + 1) * P)
                nc.tensor.matmul_mx(
                    out=bank[:, t, :], lhsT=wor_codes[:, cols].bitcast(FP8X4), lhsT_scale=wor_scales[:, cols],
                    rhs=codes[:].bitcast(FP8X4), rhs_scale=scales[:], start=True, stop=True,
                )
            return bank

        fo1 = [make_fo1(0), make_fo1(1)]
        wor_codes, wor_scales = quantize_weight(wor_dealt, "wor")
        yo = [last_layer(0, fo1[0]), last_layer(1, fo1[1])]

        y_codes = sb.tile([P, J], U32, name="y_codes", align_bytes=64)
        y_scales = sb.tile([P, J], U8, name="y_scales", align_bytes=64)
        out_rows = out_0.rearrange("(p t) j -> p t j", t=PACK)
        out_words = out_1[0].rearrange("p c t -> p (c t)").bitcast(I32)
        y_words = []
        for half in range(2):
            cols = slice(half * HALF, (half + 1) * HALF)
            woven = sb.tile([P, HALF, PACK], BF16, name="y_words" + str(half), align_bytes=64)
            y = sb.tile([P, PACK, HALF], F32, name="y" + str(half), align_bytes=64)
            nc.vector.tensor_tensor(out=y[:], in0=yo[half][:], in1=res_t[:, :, cols], op=ALU.add)
            nc.sync.dma_start(out=out_rows[:, :, cols], in_=y[:])
            weave(woven, y)
            y_words.append(woven)
        for half in range(2):
            cols = slice(half * HALF, (half + 1) * HALF)
            nc.vector.quantize_mx(
                out=y_codes[:, cols].bitcast(FP8X4), scales=y_scales[:, cols],
                in_=y_words[half][:].rearrange("p c t -> p (c t)"),
            )
            nc.sync.dma_start(out=out_words[:, cols], in_=y_codes[:, cols].bitcast(I32))
        for quad in range(4):
            queue = nc.sync if quad % 2 == 0 else nc.scalar
            queue.dma_start(
                out=out_2[0, 4 * quad : 4 * quad + 4, :].bitcast(I32),
                in_=y_scales[32 * quad : 32 * quad + 4, :].bitcast(I32),
            )
